import numpy as np
import ml_dtypes


def mxq(x, axis, fmt="e4m3"):
    dtype, down = {"e4m3": (ml_dtypes.float8_e4m3fn, 7), "e5m2": (ml_dtypes.float8_e5m2, 14)}[fmt]
    v = np.moveaxis(np.asarray(x, np.float32).astype(ml_dtypes.bfloat16).astype(np.float64), axis, -1)
    blocks = v.reshape(v.shape[:-1] + (-1, 32))
    amax = np.abs(blocks).max(-1, keepdims=True)
    byte = np.maximum(np.where(amax > 0, np.frexp(amax)[1] - 1 + 127, 0) - down, 1)
    scale = np.exp2(byte - 127.0)
    codes = (blocks / scale).astype(np.float32).astype(dtype).astype(np.float64)
    return np.moveaxis((codes * scale).reshape(v.shape), -1, axis)


WIDE = False


def mx_kscale(k):
    if not WIDE:
        return np.ones(k)
    levels = np.array([10, -10, 5, -5, 0])
    if k % 512:
        return np.exp2(np.random.permutation(np.resize(levels, k // 32))).repeat(32)
    a = np.empty((k // 512, 16))
    for p in range(k // 512):
        a[p, :8] = np.random.permutation(np.resize(levels, 8))
        for g in range(8):
            far = levels[np.abs(levels - a[p, g]) >= 10]
            a[p, g + 8] = far[np.random.randint(len(far))]
    return np.exp2(a.ravel()).repeat(32)


def f64(x):
    return np.asarray(x).astype(np.float64)


def striped(idx):
    return np.tile(idx.reshape(-1, 16).T, (8, 1)).astype(np.uint16)


def unstriped(offs):
    return offs[:16].T.reshape(-1).astype(np.int64)


E2M1 = np.array([0.0, 0.5, 1.0, 1.5, 2.0, 3.0, 4.0, 6.0, -0.0, -0.5, -1.0, -1.5, -2.0, -3.0, -4.0, -6.0])


def pack_weight(w, fmt):
    k, n = w.shape
    w = f64(np.asarray(w, np.float32).astype(ml_dtypes.bfloat16)).reshape(k // 32, 32, n)
    amax = np.abs(w).max(1)
    if fmt == "e4m3":
        byte = np.frexp(amax)[1] - 1 + 127 - 7
    else:
        mant, ex = np.frexp(amax / 6.0)
        byte = np.where(mant > 0.5, ex, ex - 1) + 127
    byte = np.clip(np.where(amax > 0, byte, 1), 1, 254)
    scaled = (w * np.exp2(127.0 - byte)[:, None, :]).reshape(k, n).astype(np.float32)
    by_word = np.ascontiguousarray(scaled.reshape(k // 512, 128, 4, n).transpose(0, 1, 3, 2))
    if fmt == "e4m3":
        words = by_word.astype(ml_dtypes.float8_e4m3fn).view(np.uint8)
    else:
        c = by_word.astype(ml_dtypes.float4_e2m1fn).view(np.uint8) & 0xF
        words = (c[..., 0::2] | (c[..., 1::2] << 4)).reshape(k // 512, 128, 2 * n)
    return np.ascontiguousarray(words), np.ascontiguousarray(byte.astype(np.uint8).reshape(k // 512, 16, n))


def unpack_weight(words, scales, fmt):
    g, _, n = scales.shape
    words = np.ascontiguousarray(words).reshape(g, 128, n, -1)
    if fmt == "e4m3":
        vals = words.view(ml_dtypes.float8_e4m3fn).astype(np.float64)
    else:
        nib = np.empty((g, 128, n, 4), np.uint8)
        nib[..., 0::2] = words & 0xF
        nib[..., 1::2] = words >> 4
        vals = E2M1[nib]
    vals = vals * np.repeat(np.exp2(scales.astype(np.float64) - 127.0), 8, axis=1)[..., None]
    return vals.transpose(0, 1, 3, 2).reshape(g * 512, n)


def gelu(v):
    return 0.5 * v * (1.0 + np.tanh(np.sqrt(2.0 / np.pi) * (v + 0.044715 * v**3)))


K, H, N, T, S, P = 1024, 1024, 512, 4096, 1024, 512


def setup_inputs():
    n = np.random.standard_normal
    s = mx_kscale(K)[:, None]
    u = mx_kscale(H)[:, None]
    d = {}
    d["tab_words"], d["tab_scales"] = pack_weight(n((K, T)) * s, "e2m1")
    d["offs"] = striped(np.random.permutation(T)[:S])
    d["pos1"] = striped(np.random.permutation(S)[:P])
    d["pos2"] = striped(np.random.permutation(S)[:P])
    d["w1"] = (0.57 / K ** 0.5 * n((K, H)) / s).astype(np.float32)
    d["gain"] = (1.5 * np.exp(0.3 * n(H)) * u[:, 0]).astype(np.float32)
    d["w2"] = (n((H, N)) / H ** 0.5 / u).astype(np.float32)
    d["w3_words"], d["w3_scales"] = pack_weight(0.57 / H ** 0.5 * n((H, N)) / u, "e2m1")
    d["cloth"] = np.exp(0.4 * n((N, P))).astype(np.float32)
    return d


def reference(tab_words, tab_scales, offs, pos1, pos2, w1, gain, w2, w3_words, w3_scales, cloth):
    v = unpack_weight(tab_words, tab_scales, "e2m1")[:, unstriped(offs)]
    w1q = mxq(f64(w1), 0, "e4m3")
    h = np.sin(w1q.T @ v)
    pot = h[:, unstriped(pos1)]
    follow = h[:, unstriped(pos2)]
    z = f64(gain)[:, None] * (pot - follow / (1.0 + np.exp(-follow)))
    zq = mxq(z, 0, "e4m3")
    w2q = mxq(f64(w2), 0, "e4m3")
    w3 = unpack_weight(w3_words, w3_scales, "e2m1")
    run = (w2q.T @ zq) * f64(cloth)
    angle = w3.T @ zq
    return run * np.cos(angle)

@@ -1,0 +1,287 @@
+import math
+from contextlib import ExitStack
+
+import concourse.mybir as mybir
+
+K, H, N, T, S, M = 1024, 1024, 512, 4096, 1024, 512
+FLOPS = 2 * K * H * S + 2 * 2 * H * N * M
+
+F32 = mybir.dt.float32
+BF16 = mybir.dt.bfloat16
+I32 = mybir.dt.int32
+U32 = mybir.dt.uint32
+U16 = mybir.dt.uint16
+U8 = mybir.dt.uint8
+FP8X4 = mybir.dt.float8_e4m3fn_x4
+FP4X4 = mybir.dt.float4_e2m1fn_x4
+ALU = mybir.AluOpType
+ACT = mybir.ActivationFunctionType
+
+P = 128
+BANK = 512
+TWO_PI = 2.0 * math.pi
+ROUNDER = 12582912.0
+TURNS = "VSVSVSVSVSVSVSVS"
+EPI = "SSVV"
+WEAVE = "SSV"
+CAST = "SSSSSS"
+GAIN = "SSSSSSSSSSSS"
+
+
+def tile_list_snooker_sequence_coach_kernel(
+    tc, tab_words, tab_scales, offs, pos1, pos2, w1, gain, w2, w3_words, w3_scales, cloth, out
+):
+    nc = tc.nc
+    with ExitStack() as ctx:
+        keep = ctx.enter_context(tc.tile_pool(name="keep", bufs=1))
+        ring = ctx.enter_context(tc.tile_pool(name="ring", bufs=4))
+        psum = ctx.enter_context(tc.psum_pool(name="psum", bufs=1))
+
+        warm = keep.tile([P, 8], F32, name="warm")
+        warm_out = keep.tile([P, 8], F32, name="warm_out")
+
+        offs_t = keep.tile([P, S // 16], U16, name="offs_t")
+        pos1_t = keep.tile([P, M // 16], U16, name="pos1_t")
+        pos2_t = keep.tile([P, M // 16], U16, name="pos2_t")
+        tab_s = keep.tile([P, T], U8, name="tab_s", align_bytes=64)
+        tab_w = [keep.tile([P, T], U16, name="tab_w%d" % a, align_bytes=64) for a in range(2)]
+        v_w = [keep.tile([P, S], U16, name="v_w%d" % a, align_bytes=64) for a in range(2)]
+        v_s = [keep.tile([P, S], U8, name="v_s%d" % a, align_bytes=64) for a in range(2)]
+        w1_raw = [[ring.tile([P, 4, BANK], F32, name="raw", bufs=2) for a in range(2)] for b in range(2)]
+        w2_raw = [ring.tile([P, 4, N], F32, name="raw", bufs=2) for a in range(2)]
+        w3_w = keep.tile([P, 2, 2 * N], U8, name="w3_w", align_bytes=64)
+        w3_s = keep.tile([P, 2, N], U8, name="w3_s", align_bytes=64)
+        gain_t = keep.tile([P, 2, 4], F32, name="gain_t")
+        cloth_t = keep.tile([P, 4, M], F32, name="cloth_t")
+
+        nc.vector.memset(tab_s[:, 0:2560].bitcast(I32), 0)
+        nc.gpsimd.memset(tab_s[:, 2560:T].bitcast(I32), 0)
+        nc.gpsimd.memset(v_s[1][:].bitcast(I32), 0)
+        nc.gpsimd.memset(w3_s[:].rearrange("p a c -> p (a c)").bitcast(I32), 0)
+
+        nc.vector.memset(warm[:], 0.0)
+        nc.scalar.activation(warm_out[:], warm[:], ACT.Silu)
+
+        def load_w1(b, a):
+            rows = w1[512 * a : 512 * (a + 1), BANK * b : BANK * (b + 1)]
+            nc.sync.dma_start(w1_raw[b][a][:], rows.rearrange("(p j) c -> p j c", j=4))
+
+        nc.sync.dma_start(offs_t[:], offs)
+        for q in range(4):
+            nc.sync.dma_start(
+                tab_s[32 * q : 32 * q + 8, :].bitcast(I32), tab_scales[:, 4 * q : 4 * q + 4, :].bitcast(I32)
+            )
+        for a in range(2):
+            load_w1(0, a)
+            nc.sync.dma_start(tab_w[a][:].bitcast(I32), tab_words[a].bitcast(I32))
+        nc.sync.dma_start(pos1_t[:], pos1)
+        nc.sync.dma_start(pos2_t[:], pos2)
+        nc.sync.dma_start(gain_t[:], gain.rearrange("(a p t) -> p a t", a=2, t=4))
+        nc.vector.tensor_copy(v_s[0][:], tab_s[:].indirect(offs_t[:]))
+        nc.sync.dma_start(v_s[1][0 : P - 4, :].bitcast(I32), v_s[0][4:P, :].bitcast(I32))
+
+
+        def codes_and_scales(name, width):
+            codes = keep.tile([P, width], U32, name=name + "_c", align_bytes=64)
+            scales = keep.tile([P, width], U8, name=name + "_s", align_bytes=64)
+            return codes, scales
+
+        w1_q = [[codes_and_scales("w1q%d%d" % (b, a), BANK) for a in range(2)] for b in range(2)]
+        w2_q = [codes_and_scales("w2q%d" % a, N) for a in range(2)]
+        z_q = [codes_and_scales("zq%d" % a, M) for a in range(2)]
+
+        def cast(which, dst, src):
+            if which == "S":
+                for c0 in range(0, dst.shape[1], 32):
+                    nc.scalar.copy(dst[:, c0 : c0 + 32], src[:, c0 : c0 + 32])
+            elif which == "V":
+                nc.vector.tensor_copy(dst, src)
+            elif which == "H":
+                cut = 48
+                nc.scalar.copy(dst[:, :cut], src[:, :cut])
+                nc.vector.tensor_copy(dst[:, cut:], src[:, cut:])
+            else:
+                for c0 in range(0, dst.shape[1], 32):
+                    nc.gpsimd.tensor_scalar(dst[:, c0 : c0 + 32], src[:, c0 : c0 + 32], 1.0, 0.0, ALU.mult, ALU.add)
+
+        def round_w1(b, a):
+            grouped = ring.tile([P, 4 * BANK], BF16, name="grouped", align_bytes=64)
+            cast(
+                CAST[2 * b + a],
+                grouped[:].rearrange("p (t m j) -> p m j t", t=4, j=4),
+                w1_raw[b][a][:].rearrange("p j (m t) -> p m j t", t=4),
+            )
+            return grouped
+
+        def round_w2(a):
+            grouped = ring.tile([P, 4 * N], BF16, name="grouped", align_bytes=64)
+            cast(
+                CAST[4 + a],
+                grouped[:].rearrange("p (c i j) -> p c j i", i=4, j=4),
+                w2_raw[a][:].rearrange("p j (c i) -> p c j i", i=4),
+            )
+            return grouped
+
+        def quantize(q, cols, grouped):
+            nc.vector.quantize_mx(out=q[0][:, cols].bitcast(FP8X4), scales=q[1][:, cols], in_=grouped)
+
+        for a in range(2):
+            quantize(w1_q[0][a], slice(0, BANK), round_w1(0, a)[:])
+        for half in range(2):
+            for a in range(2):
+                nc.vector.tensor_copy(
+                    v_w[a][:, BANK * half : BANK * (half + 1)],
+                    tab_w[a][:].indirect(offs_t[:, 32 * half : 32 * (half + 1)]),
+                )
+
+        load_w1(1, 0)
+        load_w1(1, 1)
+        for q in range(4):
+            nc.sync.dma_start(
+                w3_s[32 * q : 32 * q + 4, :, :].bitcast(I32),
+                w3_scales[:, 4 * q : 4 * q + 4, :].rearrange("a r c -> r a c").bitcast(I32),
+            )
+        nc.sync.dma_start(w3_w[:].bitcast(I32), w3_words.rearrange("a p c -> p a c").bitcast(I32))
+        nc.sync.dma_start(cloth_t[:], cloth.rearrange("(g p) m -> p g m", p=P))
+
+        def reduced_angle(bank, quarter, mode):
+            rest = ring.tile([P, BANK], F32, name="rest")
+            if mode == "G":
+                plain = ring.tile([P, BANK], F32, name="plain")
+                turns = ring.tile([P, BANK], I32, name="turns_i")
+                nc.scalar.copy(plain[:], bank)
+                nc.gpsimd.tensor_scalar(turns[:], plain[:], 1.0 / TWO_PI, quarter, ALU.mult, ALU.add)
+            elif mode == "S":
+                lifted = ring.tile([P, BANK], U32, name="lifted")
+                turns = ring.tile([P, BANK], F32, name="turns_f")
+                nc.scalar.activation(lifted[:], bank, ACT.Copy, scale=1.0 / TWO_PI, bias=ROUNDER)
+                nc.scalar.activation(turns[:], lifted[:], ACT.Copy, bias=-ROUNDER)
+            else:
+                turns = ring.tile([P, BANK], I32, name="turns_i")
+                nc.vector.tensor_scalar(turns[:], bank, 1.0 / TWO_PI, quarter, ALU.mult, ALU.add)
+            nc.vector.scalar_tensor_tensor(rest[:], turns[:], -TWO_PI, bank, ALU.mult, ALU.add)
+            return rest
+
+        def first_stage(i):
+            b, t = divmod(i, 4)
+            h = ring.tile([P, S], F32, name="h", bufs=7)
+            for half in range(2):
+                cols = slice(BANK * half, BANK * (half + 1))
+                bank = psum.tile([P, BANK], F32, name="bank", bufs=8)
+                for a in range(2):
+                    nc.tensor.matmul_mx(
+                        out=bank[:],
+                        lhsT=w1_q[b][a][0][:, P * t : P * (t + 1)].bitcast(FP8X4),
+                        lhsT_scale=w1_q[b][a][1][:, P * t : P * (t + 1)],
+                        rhs=v_w[a][:, cols].bitcast(FP4X4),
+                        rhs_scale=v_s[a][:, cols],
+                        start=(a == 0),
+                        stop=(a == 1),
+                    )
+                rest = reduced_angle(bank[:], 0.0, TURNS[2 * i + half])
+                nc.scalar.activation(h[:, cols], rest[:], ACT.Sin)
+            return h
+
+        def pick(i, h, m0, width, z_rows):
+            b, t = divmod(i, 4)
+            lists = slice(m0 // 16, (m0 + width) // 16)
+            pot = ring.tile([P, width], F32, name="pot")
+            follow = ring.tile([P, width], F32, name="follow")
+            silu = ring.tile([P, width], F32, name="silu")
+            diff = ring.tile([P, width], F32, name="diff")
+            nc.vector.tensor_copy(follow[:], h[:].indirect(pos2_t[:, lists]))
+            nc.vector.tensor_copy(pot[:], h[:].indirect(pos1_t[:, lists]))
+            nc.scalar.activation(silu[:], follow[:], ACT.Silu)
+            nc.vector.tensor_tensor(diff[:], pot[:], silu[:], ALU.subtract)
+            which = GAIN[i if m0 == 0 else i + 4]
+            if which == "S":
+                nc.scalar.activation(z_rows[:, t, :], diff[:], ACT.Copy, scale=gain_t[:, b, t : t + 1])
+            elif which == "V":
+                nc.vector.tensor_scalar(z_rows[:, t, :], diff[:], gain_t[:, b, t : t + 1], None, ALU.mult)
+            else:
+                nc.gpsimd.tensor_scalar(z_rows[:, t, :], diff[:], gain_t[:, b, t : t + 1], 0.0, ALU.mult, ALU.add)
+
+        def quantize_z(b, m0, width, z_rows):
+            grouped = ring.tile([P, 4 * width], BF16, name="grouped", align_bytes=64)
+            cast(
+                WEAVE[b + m0 // width],
+                grouped[:].rearrange("p (c i t) -> p c t i", i=4, t=4),
+                z_rows[:].rearrange("p t (c i) -> p c t i", i=4),
+            )
+            quantize(z_q[b], slice(m0, m0 + width), grouped[:])
+
+        def second_stage(m0, width):
+            for pair in range(2):
+                angle = psum.tile([P, 2, width], F32, name="bank", bufs=8)
+                run = psum.tile([P, 2, width], F32, name="bank", bufs=8)
+                for g in range(2):
+                    n0 = P * (2 * pair + g)
+                    for c0 in range(0, width, P):
+                        for a in range(2):
+                            nc.tensor.matmul_mx(
+                                out=angle[:, g, c0 : c0 + P],
+                                lhsT=w3_w[:, a, 2 * n0 : 2 * (n0 + P)].bitcast(FP4X4),
+                                lhsT_scale=w3_s[:, a, n0 : n0 + P],
+                                rhs=z_q[a][0][:, m0 + c0 : m0 + c0 + P].bitcast(FP8X4),
+                                rhs_scale=z_q[a][1][:, m0 + c0 : m0 + c0 + P],
+                                start=(a == 0),
+                                stop=(a == 1),
+                            )
+                for g in range(2):
+                    n0 = P * (2 * pair + g)
+                    for a in range(2):
+                        nc.tensor.matmul_mx(
+                            out=run[:, g, :],
+                            lhsT=w2_q[a][0][:, n0 : n0 + P].bitcast(FP8X4),
+                            lhsT_scale=w2_q[a][1][:, n0 : n0 + P],
+                            rhs=z_q[a][0][:, m0 : m0 + width].bitcast(FP8X4),
+                            rhs_scale=z_q[a][1][:, m0 : m0 + width],
+                            start=(a == 0),
+                            stop=(a == 1),
+                        )
+                mode = EPI[2 * (m0 // width) + pair]
+                rest = reduced_angle(angle[:].rearrange("p g m -> p (g m)"), 0.25 if mode == "V" else 0.0, mode)
+                cosine = ring.tile([P, 2, width], F32, name="cosine")
+                scaled = ring.tile([P, 2, width], F32, name="scaled")
+                result = ring.tile([P, 2, width], F32, name="result")
+                flat = "p g m -> p (g m)"
+                cloth_part = cloth_t[:, 2 * pair : 2 * pair + 2, m0 : m0 + width]
+                nc.vector.tensor_tensor(scaled[:], run[:], cloth_part, ALU.mult)
+                if mode == "V":
+                    nc.scalar.activation(cosine[:].rearrange(flat), rest[:], ACT.Sin, bias=math.pi / 2)
+                else:
+                    half_sine = ring.tile([P, BANK], F32, name="half_sine")
+                    squared = ring.tile([P, BANK], F32, name="squared")
+                    nc.scalar.activation(half_sine[:], rest[:], ACT.Sin, scale=0.5)
+                    nc.scalar.activation(squared[:], half_sine[:], ACT.Square)
+                    nc.scalar.activation(cosine[:].rearrange(flat), squared[:], ACT.Copy, scale=-2.0, bias=1.0)
+                nc.vector.tensor_tensor(result[:], scaled[:], cosine[:], ALU.mult)
+                rows = out[2 * P * pair : 2 * P * (pair + 1), m0 : m0 + width]
+                nc.sync.dma_start(rows.rearrange("(g p) m -> p g m", p=P), result[:])
+
+        half_m = M // 2
+        z_rows0 = keep.tile([P, 4, M], BF16, name="z_rows0")
+        z_rows1 = [keep.tile([P, 4, half_m], BF16, name="z_rows1%d" % u) for u in range(2)]
+        hs = [first_stage(0), first_stage(1)]
+        for i in range(8):
+            if i in (0, 1):
+                quantize(w1_q[1][i], slice(0, BANK), round_w1(1, i)[:])
+                rows = w2[512 * i : 512 * (i + 1), :]
+                nc.sync.dma_start(w2_raw[i][:], rows.rearrange("(p j) c -> p j c", j=4))
+            if i + 2 < 8:
+                hs.append(first_stage(i + 2))
+            if i < 4:
+                pick(i, hs[i], 0, M, z_rows0)
+            else:
+                pick(i, hs[i], 0, half_m, z_rows1[0])
+            if i == 5:
+                quantize_z(0, 0, M, z_rows0)
+            if i in (3, 4):
+                quantize(w2_q[i - 3], slice(0, N), round_w2(i - 3)[:])
+        pick(4, hs[4], half_m, half_m, z_rows1[1])
+        quantize_z(1, 0, half_m, z_rows1[0])
+        for i in range(5, 8):
+            pick(i, hs[i], half_m, half_m, z_rows1[1])
+        second_stage(0, half_m)
+        quantize_z(1, half_m, half_m, z_rows1[1])
+        second_stage(half_m, half_m)

@@ -2,6 +2,7 @@ import math
 from contextlib import ExitStack
 
 import concourse.mybir as mybir
+from concourse.masks import make_identity
 
 K, H, N, T, S, M = 1024, 1024, 512, 4096, 1024, 512
 FLOPS = 2 * K * H * S + 2 * 2 * H * N * M
@@ -21,10 +22,10 @@ P = 128
 BANK = 512
 TWO_PI = 2.0 * math.pi
 ROUNDER = 12582912.0
-TURNS = "VSVSVSVSVSVSVSVS"
-EPI = "SSVV"
+TURNS = "VSVSVSVS"
+EPI = "SSSV"
 WEAVE = "SSV"
-CAST = "SSSSSS"
+CAST = "SHHSSS"
 GAIN = "SSSSSSSSSSSS"
 
 
@@ -34,7 +35,7 @@ def tile_list_snooker_sequence_coach_kernel(
     nc = tc.nc
     with ExitStack() as ctx:
         keep = ctx.enter_context(tc.tile_pool(name="keep", bufs=1))
-        ring = ctx.enter_context(tc.tile_pool(name="ring", bufs=4))
+        ring = ctx.enter_context(tc.tile_pool(name="ring", bufs=3))
         psum = ctx.enter_context(tc.psum_pool(name="psum", bufs=1))
 
         warm = keep.tile([P, 8], F32, name="warm")
@@ -62,6 +63,11 @@ def tile_list_snooker_sequence_coach_kernel(
         nc.vector.memset(warm[:], 0.0)
         nc.scalar.activation(warm_out[:], warm[:], ACT.Silu)
 
+        ident = keep.tile([P, P], F32, name="ident")
+        unlift = keep.tile([P, P], F32, name="unlift")
+        make_identity(nc, ident[:])
+        nc.gpsimd.memset(unlift[:], -ROUNDER)
+
         def load_w1(b, a):
             rows = w1[512 * a : 512 * (a + 1), BANK * b : BANK * (b + 1)]
             nc.sync.dma_start(w1_raw[b][a][:], rows.rearrange("(p j) c -> p j c", j=4))
@@ -71,14 +77,15 @@ def tile_list_snooker_sequence_coach_kernel(
             nc.sync.dma_start(
                 tab_s[32 * q : 32 * q + 8, :].bitcast(I32), tab_scales[:, 4 * q : 4 * q + 4, :].bitcast(I32)
             )
-        for a in range(2):
-            load_w1(0, a)
-            nc.sync.dma_start(tab_w[a][:].bitcast(I32), tab_words[a].bitcast(I32))
+        nc.sync.dma_start(tab_w[0][:].bitcast(I32), tab_words[0].bitcast(I32))
+        load_w1(0, 0)
+        load_w1(0, 1)
+        nc.sync.dma_start(tab_w[1][:].bitcast(I32), tab_words[1].bitcast(I32))
         nc.sync.dma_start(pos1_t[:], pos1)
         nc.sync.dma_start(pos2_t[:], pos2)
         nc.sync.dma_start(gain_t[:], gain.rearrange("(a p t) -> p a t", a=2, t=4))
         nc.vector.tensor_copy(v_s[0][:], tab_s[:].indirect(offs_t[:]))
-        nc.sync.dma_start(v_s[1][0 : P - 4, :].bitcast(I32), v_s[0][4:P, :].bitcast(I32))
+        nc.sync.dma_start(v_s[1][0:100, :].bitcast(I32), v_s[0][4:104, :].bitcast(I32))
 
 
         def codes_and_scales(name, width):
@@ -97,7 +104,7 @@ def tile_list_snooker_sequence_coach_kernel(
             elif which == "V":
                 nc.vector.tensor_copy(dst, src)
             elif which == "H":
-                cut = 48
+                cut = 64
                 nc.scalar.copy(dst[:, :cut], src[:, :cut])
                 nc.vector.tensor_copy(dst[:, cut:], src[:, cut:])
             else:
@@ -145,26 +152,28 @@ def tile_list_snooker_sequence_coach_kernel(
         nc.sync.dma_start(cloth_t[:], cloth.rearrange("(g p) m -> p g m", p=P))
 
         def reduced_angle(bank, quarter, mode):
-            rest = ring.tile([P, BANK], F32, name="rest")
+            rest = ring.tile([P, BANK], F32, name="rest", bufs=5)
             if mode == "G":
                 plain = ring.tile([P, BANK], F32, name="plain")
-                turns = ring.tile([P, BANK], I32, name="turns_i")
+                turns = ring.tile([P, BANK], I32, name="turns_k", bufs=5)
                 nc.scalar.copy(plain[:], bank)
                 nc.gpsimd.tensor_scalar(turns[:], plain[:], 1.0 / TWO_PI, quarter, ALU.mult, ALU.add)
             elif mode == "S":
-                lifted = ring.tile([P, BANK], U32, name="lifted")
-                turns = ring.tile([P, BANK], F32, name="turns_f")
+                lifted = ring.tile([P, BANK], U32, name="lifted", bufs=2)
+                turns = ring.tile([P, BANK], F32, name="turns_k", bufs=5)
                 nc.scalar.activation(lifted[:], bank, ACT.Copy, scale=1.0 / TWO_PI, bias=ROUNDER)
                 nc.scalar.activation(turns[:], lifted[:], ACT.Copy, bias=-ROUNDER)
             else:
-                turns = ring.tile([P, BANK], I32, name="turns_i")
+                turns = ring.tile([P, BANK], I32, name="turns_k", bufs=5)
                 nc.vector.tensor_scalar(turns[:], bank, 1.0 / TWO_PI, quarter, ALU.mult, ALU.add)
             nc.vector.scalar_tensor_tensor(rest[:], turns[:], -TWO_PI, bank, ALU.mult, ALU.add)
-            return rest
+            return rest, turns
 
-        def first_stage(i):
+        spent = {}
+
+        def direct_stage(i):
             b, t = divmod(i, 4)
-            h = ring.tile([P, S], F32, name="h", bufs=7)
+            h = ring.tile([P, S], F32, name="h", bufs=8)
             for half in range(2):
                 cols = slice(BANK * half, BANK * (half + 1))
                 bank = psum.tile([P, BANK], F32, name="bank", bufs=8)
@@ -178,28 +187,72 @@ def tile_list_snooker_sequence_coach_kernel(
                         start=(a == 0),
                         stop=(a == 1),
                     )
-                rest = reduced_angle(bank[:], 0.0, TURNS[2 * i + half])
+                rest, turns = reduced_angle(bank[:], 0.0, TURNS[2 * i + half])
+                spent[i, half] = rest, turns
                 nc.scalar.activation(h[:, cols], rest[:], ACT.Sin)
             return h
 
-        def pick(i, h, m0, width, z_rows):
-            b, t = divmod(i, 4)
+        def turns_of(b, pair):
+            turns = ring.tile([P, 2, BANK], F32, name="turns", bufs=4)
+            lifted = ring.tile([P, 2, BANK], F32, name="lifted2", bufs=4)
+            for e in range(2):
+                cols = slice(P * (2 * pair + e), P * (2 * pair + e + 1))
+                bank = psum.tile([P, BANK], F32, name="bank", bufs=8)
+                for a in range(2):
+                    nc.tensor.matmul_mx(
+                        out=bank[:],
+                        lhsT=v_w[a][:, cols].bitcast(FP4X4),
+                        lhsT_scale=v_s[a][:, cols],
+                        rhs=w1_q[b][a][0][:].bitcast(FP8X4),
+                        rhs_scale=w1_q[b][a][1][:],
+                        start=(a == 0),
+                        stop=(a == 1),
+                    )
+                nc.scalar.activation(turns[:, e, :], bank[:], ACT.Copy, scale=1.0 / TWO_PI)
+            flat = "p e c -> p (e c)"
+            nc.vector.tensor_scalar(lifted[:].rearrange(flat), turns[:].rearrange(flat), -1.0, ROUNDER, ALU.mult, ALU.add)
+            return turns, lifted
+
+        def sine_half(h, t, half, parts):
+            bank = psum.tile([P, BANK], F32, name="bank", bufs=8)
+            for q in range(4):
+                turns, lifted = parts[2 * half + q // 2]
+                dst = bank[:, P * q : P * (q + 1)]
+                rows = slice(P * t, P * (t + 1))
+                nc.tensor.matmul(dst, unlift[:], ident[:], start=True, stop=False, is_transpose=True)
+                nc.tensor.matmul(dst, lifted[:, q % 2, rows], ident[:], start=False, stop=False, is_transpose=True)
+                nc.tensor.matmul(dst, turns[:, q % 2, rows], ident[:], start=False, stop=True, is_transpose=True)
+            nc.scalar.activation(h[:, BANK * half : BANK * (half + 1)], bank[:], ACT.Sin, scale=TWO_PI)
+
+        def first_stage(i, parts):
+            h = ring.tile([P, S], F32, name="h", bufs=8)
+            for half in range(2):
+                sine_half(h, i % 4, half, parts)
+            return h
+
+        def gather(i, h, m0, width, into=None):
             lists = slice(m0 // 16, (m0 + width) // 16)
-            pot = ring.tile([P, width], F32, name="pot")
-            follow = ring.tile([P, width], F32, name="follow")
-            silu = ring.tile([P, width], F32, name="silu")
-            diff = ring.tile([P, width], F32, name="diff")
-            nc.vector.tensor_copy(follow[:], h[:].indirect(pos2_t[:, lists]))
-            nc.vector.tensor_copy(pot[:], h[:].indirect(pos1_t[:, lists]))
-            nc.scalar.activation(silu[:], follow[:], ACT.Silu)
-            nc.vector.tensor_tensor(diff[:], pot[:], silu[:], ALU.subtract)
-            which = GAIN[i if m0 == 0 else i + 4]
-            if which == "S":
-                nc.scalar.activation(z_rows[:, t, :], diff[:], ACT.Copy, scale=gain_t[:, b, t : t + 1])
-            elif which == "V":
-                nc.vector.tensor_scalar(z_rows[:, t, :], diff[:], gain_t[:, b, t : t + 1], None, ALU.mult)
+            pot = ring.tile([P, width], F32, name="pot", bufs=4)
+            if into is None:
+                follow = ring.tile([P, width], F32, name="follow")[:]
             else:
-                nc.gpsimd.tensor_scalar(z_rows[:, t, :], diff[:], gain_t[:, b, t : t + 1], 0.0, ALU.mult, ALU.add)
+                follow = into[:, 0:width].bitcast(F32)
+            nc.vector.tensor_copy(follow, h[:].indirect(pos2_t[:, lists]))
+            nc.vector.tensor_copy(pot[:], h[:].indirect(pos1_t[:, lists]))
+            return pot, follow
+
+        def combine(i, picked, width, z_rows, into=None):
+            b, t = divmod(i, 4)
+            pot, follow = picked
+            gain_col = gain_t[:, b, t : t + 1]
+            if into is None:
+                silu = ring.tile([P, width], F32, name="silu")[:]
+            else:
+                silu = into[:, 0:width]
+            gained = ring.tile([P, width], F32, name="gained")
+            nc.scalar.activation(silu, follow, ACT.Silu)
+            nc.scalar.activation(gained[:], silu, ACT.Copy, scale=gain_col)
+            nc.vector.scalar_tensor_tensor(z_rows[:, t, :], pot[:], gain_col, gained[:], ALU.mult, ALU.subtract)
 
         def quantize_z(b, m0, width, z_rows):
             grouped = ring.tile([P, 4 * width], BF16, name="grouped", align_bytes=64)
@@ -214,74 +267,87 @@ def tile_list_snooker_sequence_coach_kernel(
             for pair in range(2):
                 angle = psum.tile([P, 2, width], F32, name="bank", bufs=8)
                 run = psum.tile([P, 2, width], F32, name="bank", bufs=8)
-                for g in range(2):
-                    n0 = P * (2 * pair + g)
-                    for c0 in range(0, width, P):
-                        for a in range(2):
+                for a in range(2):
+                    for g in range(2):
+                        n0 = P * (2 * pair + g)
+                        for c0 in range(0, width, P):
                             nc.tensor.matmul_mx(
                                 out=angle[:, g, c0 : c0 + P],
                                 lhsT=w3_w[:, a, 2 * n0 : 2 * (n0 + P)].bitcast(FP4X4),
                                 lhsT_scale=w3_s[:, a, n0 : n0 + P],
                                 rhs=z_q[a][0][:, m0 + c0 : m0 + c0 + P].bitcast(FP8X4),
                                 rhs_scale=z_q[a][1][:, m0 + c0 : m0 + c0 + P],
-                                start=(a == 0),
-                                stop=(a == 1),
+                                start=(a == 0 and g == 0 and c0 == 0),
+                                stop=(a == 1 and g == 1 and c0 == width - P),
                             )
-                for g in range(2):
-                    n0 = P * (2 * pair + g)
-                    for a in range(2):
+                for a in range(2):
+                    for g in range(2):
+                        n0 = P * (2 * pair + g)
                         nc.tensor.matmul_mx(
                             out=run[:, g, :],
                             lhsT=w2_q[a][0][:, n0 : n0 + P].bitcast(FP8X4),
                             lhsT_scale=w2_q[a][1][:, n0 : n0 + P],
                             rhs=z_q[a][0][:, m0 : m0 + width].bitcast(FP8X4),
                             rhs_scale=z_q[a][1][:, m0 : m0 + width],
-                            start=(a == 0),
-                            stop=(a == 1),
+                            start=(a == 0 and g == 0),
+                            stop=(a == 1 and g == 1),
                         )
                 mode = EPI[2 * (m0 // width) + pair]
-                rest = reduced_angle(angle[:].rearrange("p g m -> p (g m)"), 0.25 if mode == "V" else 0.0, mode)
-                cosine = ring.tile([P, 2, width], F32, name="cosine")
-                scaled = ring.tile([P, 2, width], F32, name="scaled")
-                result = ring.tile([P, 2, width], F32, name="result")
+                rest, turns = reduced_angle(angle[:].rearrange("p g m -> p (g m)"), 0.25 if mode == "V" else 0.0, mode)
+                cosine = ring.tile([P, 2, width], F32, name="cosine", bufs=2)
+                scaled = ring.tile([P, 2, width], F32, name="scaled", bufs=2)
+                result = ring.tile([P, 2, width], F32, name="result", bufs=2)
                 flat = "p g m -> p (g m)"
                 cloth_part = cloth_t[:, 2 * pair : 2 * pair + 2, m0 : m0 + width]
                 nc.vector.tensor_tensor(scaled[:], run[:], cloth_part, ALU.mult)
                 if mode == "V":
                     nc.scalar.activation(cosine[:].rearrange(flat), rest[:], ACT.Sin, bias=math.pi / 2)
                 else:
-                    half_sine = ring.tile([P, BANK], F32, name="half_sine")
-                    squared = ring.tile([P, BANK], F32, name="squared")
-                    nc.scalar.activation(half_sine[:], rest[:], ACT.Sin, scale=0.5)
-                    nc.scalar.activation(squared[:], half_sine[:], ACT.Square)
-                    nc.scalar.activation(cosine[:].rearrange(flat), squared[:], ACT.Copy, scale=-2.0, bias=1.0)
-                nc.vector.tensor_tensor(result[:], scaled[:], cosine[:], ALU.mult)
+                    folded = ring.tile([P, BANK], F32, name="folded", bufs=2)
+                    nc.scalar.activation(folded[:], rest[:], ACT.Abs)
+                    nc.scalar.activation(cosine[:].rearrange(flat), folded[:], ACT.Sin, scale=-1.0, bias=math.pi / 2)
+                last = nc.gpsimd if "VVVV"[2 * (m0 // width) + pair] == "G" else nc.vector
+                last.tensor_tensor(result[:], scaled[:], cosine[:], ALU.mult)
                 rows = out[2 * P * pair : 2 * P * (pair + 1), m0 : m0 + width]
                 nc.sync.dma_start(rows.rearrange("(g p) m -> p g m", p=P), result[:])
 
         half_m = M // 2
         z_rows0 = keep.tile([P, 4, M], BF16, name="z_rows0")
         z_rows1 = [keep.tile([P, 4, half_m], BF16, name="z_rows1%d" % u) for u in range(2)]
-        hs = [first_stage(0), first_stage(1)]
-        for i in range(8):
-            if i in (0, 1):
-                quantize(w1_q[1][i], slice(0, BANK), round_w1(1, i)[:])
-                rows = w2[512 * i : 512 * (i + 1), :]
-                nc.sync.dma_start(w2_raw[i][:], rows.rearrange("(p j) c -> p j c", j=4))
-            if i + 2 < 8:
-                hs.append(first_stage(i + 2))
-            if i < 4:
-                pick(i, hs[i], 0, M, z_rows0)
-            else:
-                pick(i, hs[i], 0, half_m, z_rows1[0])
-            if i == 5:
+        hs = [direct_stage(0)]
+        for a in range(2):
+            quantize(w1_q[1][a], slice(0, BANK), round_w1(1, a)[:])
+            rows = w2[512 * a : 512 * (a + 1), :]
+            nc.sync.dma_start(w2_raw[a][:], rows.rearrange("(p j) c -> p j c", j=4))
+        hs.append(direct_stage(1))
+        parts = [turns_of(1, pair) for pair in range(4)]
+        picked = {}
+        for i in range(8 + 1):
+            if i < 8:
+                width = M if i < 4 else half_m
+                hold = spent[i + 1, 1][1] if True and 1 <= i < 3 else None
+                picked[i] = gather(i, hs[i], 0, width, hold)
+            if i + 2 < 4:
+                hs.append(direct_stage(i + 2))
+            for j in {2: (4,), 3: (5,), 4: (6,), 5: (7,)}.get(i, ()):
+                hs.append(first_stage(j, parts))
+            n = i - 1
+            if n >= 0:
+                width = M if n < 4 else half_m
+                hold = spent[n + 2, 0][0] if True and n + 2 < 4 else None
+                combine(n, picked[n], width, z_rows0 if n < 4 else z_rows1[0], hold)
+            if n == 6:
                 quantize_z(0, 0, M, z_rows0)
-            if i in (3, 4):
-                quantize(w2_q[i - 3], slice(0, N), round_w2(i - 3)[:])
-        pick(4, hs[4], half_m, half_m, z_rows1[1])
+            if i in (7, 8):
+                quantize(w2_q[i - 7], slice(0, N), round_w2(i - 7)[:])
+            if i >= 7:
+                late = i - 3
+                picked[late, 1] = gather(late, hs[late], half_m, half_m)
         quantize_z(1, 0, half_m, z_rows1[0])
-        for i in range(5, 8):
-            pick(i, hs[i], half_m, half_m, z_rows1[1])
+        for i in range(4, 8):
+            if (i, 1) not in picked:
+                picked[i, 1] = gather(i, hs[i], half_m, half_m)
+            combine(i, picked[i, 1], half_m, z_rows1[1])
         second_stage(0, half_m)
         quantize_z(1, half_m, half_m, z_rows1[1])
         second_stage(half_m, half_m)

import math
from contextlib import ExitStack

import concourse.mybir as mybir
from concourse.masks import make_identity

K, H, N, T, S, M = 1024, 1024, 512, 4096, 1024, 512
FLOPS = 2 * K * H * S + 2 * 2 * H * N * M

F32 = mybir.dt.float32
BF16 = mybir.dt.bfloat16
I32 = mybir.dt.int32
U32 = mybir.dt.uint32
U16 = mybir.dt.uint16
U8 = mybir.dt.uint8
FP8X4 = mybir.dt.float8_e4m3fn_x4
FP4X4 = mybir.dt.float4_e2m1fn_x4
ALU = mybir.AluOpType
ACT = mybir.ActivationFunctionType

P = 128
BANK = 512
TWO_PI = 2.0 * math.pi
ROUNDER = 12582912.0
TURNS = "VSVSVSVS"
EPI = "SSSV"
WEAVE = "SSV"
CAST = "SHHSSS"
GAIN = "SSSSSSSSSSSS"


def tile_list_snooker_sequence_coach_kernel(
    tc, tab_words, tab_scales, offs, pos1, pos2, w1, gain, w2, w3_words, w3_scales, cloth, out
):
    nc = tc.nc
    with ExitStack() as ctx:
        keep = ctx.enter_context(tc.tile_pool(name="keep", bufs=1))
        ring = ctx.enter_context(tc.tile_pool(name="ring", bufs=3))
        psum = ctx.enter_context(tc.psum_pool(name="psum", bufs=1))

        warm = keep.tile([P, 8], F32, name="warm")
        warm_out = keep.tile([P, 8], F32, name="warm_out")

        offs_t = keep.tile([P, S // 16], U16, name="offs_t")
        pos1_t = keep.tile([P, M // 16], U16, name="pos1_t")
        pos2_t = keep.tile([P, M // 16], U16, name="pos2_t")
        tab_s = keep.tile([P, T], U8, name="tab_s", align_bytes=64)
        tab_w = [keep.tile([P, T], U16, name="tab_w%d" % a, align_bytes=64) for a in range(2)]
        v_w = [keep.tile([P, S], U16, name="v_w%d" % a, align_bytes=64) for a in range(2)]
        v_s = [keep.tile([P, S], U8, name="v_s%d" % a, align_bytes=64) for a in range(2)]
        w1_raw = [[ring.tile([P, 4, BANK], F32, name="raw", bufs=2) for a in range(2)] for b in range(2)]
        w2_raw = [ring.tile([P, 4, N], F32, name="raw", bufs=2) for a in range(2)]
        w3_w = keep.tile([P, 2, 2 * N], U8, name="w3_w", align_bytes=64)
        w3_s = keep.tile([P, 2, N], U8, name="w3_s", align_bytes=64)
        gain_t = keep.tile([P, 2, 4], F32, name="gain_t")
        cloth_t = keep.tile([P, 4, M], F32, name="cloth_t")

        nc.vector.memset(tab_s[:, 0:2560].bitcast(I32), 0)
        nc.gpsimd.memset(tab_s[:, 2560:T].bitcast(I32), 0)
        nc.gpsimd.memset(v_s[1][:].bitcast(I32), 0)
        nc.gpsimd.memset(w3_s[:].rearrange("p a c -> p (a c)").bitcast(I32), 0)

        nc.vector.memset(warm[:], 0.0)
        nc.scalar.activation(warm_out[:], warm[:], ACT.Silu)

        ident = keep.tile([P, P], F32, name="ident")
        unlift = keep.tile([P, P], F32, name="unlift")
        make_identity(nc, ident[:])
        nc.gpsimd.memset(unlift[:], -ROUNDER)

        def load_w1(b, a):
            rows = w1[512 * a : 512 * (a + 1), BANK * b : BANK * (b + 1)]
            nc.sync.dma_start(w1_raw[b][a][:], rows.rearrange("(p j) c -> p j c", j=4))

        nc.sync.dma_start(offs_t[:], offs)
        for q in range(4):
            nc.sync.dma_start(
                tab_s[32 * q : 32 * q + 8, :].bitcast(I32), tab_scales[:, 4 * q : 4 * q + 4, :].bitcast(I32)
            )
        nc.sync.dma_start(tab_w[0][:].bitcast(I32), tab_words[0].bitcast(I32))
        load_w1(0, 0)
        load_w1(0, 1)
        nc.sync.dma_start(tab_w[1][:].bitcast(I32), tab_words[1].bitcast(I32))
        nc.sync.dma_start(pos1_t[:], pos1)
        nc.sync.dma_start(pos2_t[:], pos2)
        nc.sync.dma_start(gain_t[:], gain.rearrange("(a p t) -> p a t", a=2, t=4))
        nc.vector.tensor_copy(v_s[0][:], tab_s[:].indirect(offs_t[:]))
        nc.sync.dma_start(v_s[1][0:100, :].bitcast(I32), v_s[0][4:104, :].bitcast(I32))


        def codes_and_scales(name, width):
            codes = keep.tile([P, width], U32, name=name + "_c", align_bytes=64)
            scales = keep.tile([P, width], U8, name=name + "_s", align_bytes=64)
            return codes, scales

        w1_q = [[codes_and_scales("w1q%d%d" % (b, a), BANK) for a in range(2)] for b in range(2)]
        w2_q = [codes_and_scales("w2q%d" % a, N) for a in range(2)]
        z_q = [codes_and_scales("zq%d" % a, M) for a in range(2)]

        def cast(which, dst, src):
            if which == "S":
                for c0 in range(0, dst.shape[1], 32):
                    nc.scalar.copy(dst[:, c0 : c0 + 32], src[:, c0 : c0 + 32])
            elif which == "V":
                nc.vector.tensor_copy(dst, src)
            elif which == "H":
                cut = 64
                nc.scalar.copy(dst[:, :cut], src[:, :cut])
                nc.vector.tensor_copy(dst[:, cut:], src[:, cut:])
            else:
                for c0 in range(0, dst.shape[1], 32):
                    nc.gpsimd.tensor_scalar(dst[:, c0 : c0 + 32], src[:, c0 : c0 + 32], 1.0, 0.0, ALU.mult, ALU.add)

        def round_w1(b, a):
            grouped = ring.tile([P, 4 * BANK], BF16, name="grouped", align_bytes=64)
            cast(
                CAST[2 * b + a],
                grouped[:].rearrange("p (t m j) -> p m j t", t=4, j=4),
                w1_raw[b][a][:].rearrange("p j (m t) -> p m j t", t=4),
            )
            return grouped

        def round_w2(a):
            grouped = ring.tile([P, 4 * N], BF16, name="grouped", align_bytes=64)
            cast(
                CAST[4 + a],
                grouped[:].rearrange("p (c i j) -> p c j i", i=4, j=4),
                w2_raw[a][:].rearrange("p j (c i) -> p c j i", i=4),
            )
            return grouped

        def quantize(q, cols, grouped):
            nc.vector.quantize_mx(out=q[0][:, cols].bitcast(FP8X4), scales=q[1][:, cols], in_=grouped)

        for a in range(2):
            quantize(w1_q[0][a], slice(0, BANK), round_w1(0, a)[:])
        for half in range(2):
            for a in range(2):
                nc.vector.tensor_copy(
                    v_w[a][:, BANK * half : BANK * (half + 1)],
                    tab_w[a][:].indirect(offs_t[:, 32 * half : 32 * (half + 1)]),
                )

        load_w1(1, 0)
        load_w1(1, 1)
        for q in range(4):
            nc.sync.dma_start(
                w3_s[32 * q : 32 * q + 4, :, :].bitcast(I32),
                w3_scales[:, 4 * q : 4 * q + 4, :].rearrange("a r c -> r a c").bitcast(I32),
            )
        nc.sync.dma_start(w3_w[:].bitcast(I32), w3_words.rearrange("a p c -> p a c").bitcast(I32))
        nc.sync.dma_start(cloth_t[:], cloth.rearrange("(g p) m -> p g m", p=P))

        def reduced_angle(bank, quarter, mode):
            rest = ring.tile([P, BANK], F32, name="rest", bufs=5)
            if mode == "G":
                plain = ring.tile([P, BANK], F32, name="plain")
                turns = ring.tile([P, BANK], I32, name="turns_k", bufs=5)
                nc.scalar.copy(plain[:], bank)
                nc.gpsimd.tensor_scalar(turns[:], plain[:], 1.0 / TWO_PI, quarter, ALU.mult, ALU.add)
            elif mode == "S":
                lifted = ring.tile([P, BANK], U32, name="lifted", bufs=2)
                turns = ring.tile([P, BANK], F32, name="turns_k", bufs=5)
                nc.scalar.activation(lifted[:], bank, ACT.Copy, scale=1.0 / TWO_PI, bias=ROUNDER)
                nc.scalar.activation(turns[:], lifted[:], ACT.Copy, bias=-ROUNDER)
            else:
                turns = ring.tile([P, BANK], I32, name="turns_k", bufs=5)
                nc.vector.tensor_scalar(turns[:], bank, 1.0 / TWO_PI, quarter, ALU.mult, ALU.add)
            nc.vector.scalar_tensor_tensor(rest[:], turns[:], -TWO_PI, bank, ALU.mult, ALU.add)
            return rest, turns

        spent = {}

        def direct_stage(i):
            b, t = divmod(i, 4)
            h = ring.tile([P, S], F32, name="h", bufs=8)
            for half in range(2):
                cols = slice(BANK * half, BANK * (half + 1))
                bank = psum.tile([P, BANK], F32, name="bank", bufs=8)
                for a in range(2):
                    nc.tensor.matmul_mx(
                        out=bank[:],
                        lhsT=w1_q[b][a][0][:, P * t : P * (t + 1)].bitcast(FP8X4),
                        lhsT_scale=w1_q[b][a][1][:, P * t : P * (t + 1)],
                        rhs=v_w[a][:, cols].bitcast(FP4X4),
                        rhs_scale=v_s[a][:, cols],
                        start=(a == 0),
                        stop=(a == 1),
                    )
                rest, turns = reduced_angle(bank[:], 0.0, TURNS[2 * i + half])
                spent[i, half] = rest, turns
                nc.scalar.activation(h[:, cols], rest[:], ACT.Sin)
            return h

        def turns_of(b, pair):
            turns = ring.tile([P, 2, BANK], F32, name="turns", bufs=4)
            lifted = ring.tile([P, 2, BANK], F32, name="lifted2", bufs=4)
            for e in range(2):
                cols = slice(P * (2 * pair + e), P * (2 * pair + e + 1))
                bank = psum.tile([P, BANK], F32, name="bank", bufs=8)
                for a in range(2):
                    nc.tensor.matmul_mx(
                        out=bank[:],
                        lhsT=v_w[a][:, cols].bitcast(FP4X4),
                        lhsT_scale=v_s[a][:, cols],
                        rhs=w1_q[b][a][0][:].bitcast(FP8X4),
                        rhs_scale=w1_q[b][a][1][:],
                        start=(a == 0),
                        stop=(a == 1),
                    )
                nc.scalar.activation(turns[:, e, :], bank[:], ACT.Copy, scale=1.0 / TWO_PI)
            flat = "p e c -> p (e c)"
            nc.vector.tensor_scalar(lifted[:].rearrange(flat), turns[:].rearrange(flat), -1.0, ROUNDER, ALU.mult, ALU.add)
            return turns, lifted

        def sine_half(h, t, half, parts):
            bank = psum.tile([P, BANK], F32, name="bank", bufs=8)
            for q in range(4):
                turns, lifted = parts[2 * half + q // 2]
                dst = bank[:, P * q : P * (q + 1)]
                rows = slice(P * t, P * (t + 1))
                nc.tensor.matmul(dst, unlift[:], ident[:], start=True, stop=False, is_transpose=True)
                nc.tensor.matmul(dst, lifted[:, q % 2, rows], ident[:], start=False, stop=False, is_transpose=True)
                nc.tensor.matmul(dst, turns[:, q % 2, rows], ident[:], start=False, stop=True, is_transpose=True)
            nc.scalar.activation(h[:, BANK * half : BANK * (half + 1)], bank[:], ACT.Sin, scale=TWO_PI)

        def first_stage(i, parts):
            h = ring.tile([P, S], F32, name="h", bufs=8)
            for half in range(2):
                sine_half(h, i % 4, half, parts)
            return h

        def gather(i, h, m0, width, into=None):
            lists = slice(m0 // 16, (m0 + width) // 16)
            pot = ring.tile([P, width], F32, name="pot", bufs=4)
            if into is None:
                follow = ring.tile([P, width], F32, name="follow")[:]
            else:
                follow = into[:, 0:width].bitcast(F32)
            nc.vector.tensor_copy(follow, h[:].indirect(pos2_t[:, lists]))
            nc.vector.tensor_copy(pot[:], h[:].indirect(pos1_t[:, lists]))
            return pot, follow

        def combine(i, picked, width, z_rows, into=None):
            b, t = divmod(i, 4)
            pot, follow = picked
            gain_col = gain_t[:, b, t : t + 1]
            if into is None:
                silu = ring.tile([P, width], F32, name="silu")[:]
            else:
                silu = into[:, 0:width]
            gained = ring.tile([P, width], F32, name="gained")
            nc.scalar.activation(silu, follow, ACT.Silu)
            nc.scalar.activation(gained[:], silu, ACT.Copy, scale=gain_col)
            nc.vector.scalar_tensor_tensor(z_rows[:, t, :], pot[:], gain_col, gained[:], ALU.mult, ALU.subtract)

        def quantize_z(b, m0, width, z_rows):
            grouped = ring.tile([P, 4 * width], BF16, name="grouped", align_bytes=64)
            cast(
                WEAVE[b + m0 // width],
                grouped[:].rearrange("p (c i t) -> p c t i", i=4, t=4),
                z_rows[:].rearrange("p t (c i) -> p c t i", i=4),
            )
            quantize(z_q[b], slice(m0, m0 + width), grouped[:])

        def second_stage(m0, width):
            for pair in range(2):
                angle = psum.tile([P, 2, width], F32, name="bank", bufs=8)
                run = psum.tile([P, 2, width], F32, name="bank", bufs=8)
                for a in range(2):
                    for g in range(2):
                        n0 = P * (2 * pair + g)
                        for c0 in range(0, width, P):
                            nc.tensor.matmul_mx(
                                out=angle[:, g, c0 : c0 + P],
                                lhsT=w3_w[:, a, 2 * n0 : 2 * (n0 + P)].bitcast(FP4X4),
                                lhsT_scale=w3_s[:, a, n0 : n0 + P],
                                rhs=z_q[a][0][:, m0 + c0 : m0 + c0 + P].bitcast(FP8X4),
                                rhs_scale=z_q[a][1][:, m0 + c0 : m0 + c0 + P],
                                start=(a == 0 and g == 0 and c0 == 0),
                                stop=(a == 1 and g == 1 and c0 == width - P),
                            )
                for a in range(2):
                    for g in range(2):
                        n0 = P * (2 * pair + g)
                        nc.tensor.matmul_mx(
                            out=run[:, g, :],
                            lhsT=w2_q[a][0][:, n0 : n0 + P].bitcast(FP8X4),
                            lhsT_scale=w2_q[a][1][:, n0 : n0 + P],
                            rhs=z_q[a][0][:, m0 : m0 + width].bitcast(FP8X4),
                            rhs_scale=z_q[a][1][:, m0 : m0 + width],
                            start=(a == 0 and g == 0),
                            stop=(a == 1 and g == 1),
                        )
                mode = EPI[2 * (m0 // width) + pair]
                rest, turns = reduced_angle(angle[:].rearrange("p g m -> p (g m)"), 0.25 if mode == "V" else 0.0, mode)
                cosine = ring.tile([P, 2, width], F32, name="cosine", bufs=2)
                scaled = ring.tile([P, 2, width], F32, name="scaled", bufs=2)
                result = ring.tile([P, 2, width], F32, name="result", bufs=2)
                flat = "p g m -> p (g m)"
                cloth_part = cloth_t[:, 2 * pair : 2 * pair + 2, m0 : m0 + width]
                nc.vector.tensor_tensor(scaled[:], run[:], cloth_part, ALU.mult)
                if mode == "V":
                    nc.scalar.activation(cosine[:].rearrange(flat), rest[:], ACT.Sin, bias=math.pi / 2)
                else:
                    folded = ring.tile([P, BANK], F32, name="folded", bufs=2)
                    nc.scalar.activation(folded[:], rest[:], ACT.Abs)
                    nc.scalar.activation(cosine[:].rearrange(flat), folded[:], ACT.Sin, scale=-1.0, bias=math.pi / 2)
                last = nc.gpsimd if "VVVV"[2 * (m0 // width) + pair] == "G" else nc.vector
                last.tensor_tensor(result[:], scaled[:], cosine[:], ALU.mult)
                rows = out[2 * P * pair : 2 * P * (pair + 1), m0 : m0 + width]
                nc.sync.dma_start(rows.rearrange("(g p) m -> p g m", p=P), result[:])

        half_m = M // 2
        z_rows0 = keep.tile([P, 4, M], BF16, name="z_rows0")
        z_rows1 = [keep.tile([P, 4, half_m], BF16, name="z_rows1%d" % u) for u in range(2)]
        hs = [direct_stage(0)]
        for a in range(2):
            quantize(w1_q[1][a], slice(0, BANK), round_w1(1, a)[:])
            rows = w2[512 * a : 512 * (a + 1), :]
            nc.sync.dma_start(w2_raw[a][:], rows.rearrange("(p j) c -> p j c", j=4))
        hs.append(direct_stage(1))
        parts = [turns_of(1, pair) for pair in range(4)]
        picked = {}
        for i in range(8 + 1):
            if i < 8:
                width = M if i < 4 else half_m
                hold = spent[i + 1, 1][1] if True and 1 <= i < 3 else None
                picked[i] = gather(i, hs[i], 0, width, hold)
            if i + 2 < 4:
                hs.append(direct_stage(i + 2))
            for j in {2: (4,), 3: (5,), 4: (6,), 5: (7,)}.get(i, ()):
                hs.append(first_stage(j, parts))
            n = i - 1
            if n >= 0:
                width = M if n < 4 else half_m
                hold = spent[n + 2, 0][0] if True and n + 2 < 4 else None
                combine(n, picked[n], width, z_rows0 if n < 4 else z_rows1[0], hold)
            if n == 6:
                quantize_z(0, 0, M, z_rows0)
            if i in (7, 8):
                quantize(w2_q[i - 7], slice(0, N), round_w2(i - 7)[:])
            if i >= 7:
                late = i - 3
                picked[late, 1] = gather(late, hs[late], half_m, half_m)
        quantize_z(1, 0, half_m, z_rows1[0])
        for i in range(4, 8):
            if (i, 1) not in picked:
                picked[i, 1] = gather(i, hs[i], half_m, half_m)
            combine(i, picked[i, 1], half_m, z_rows1[1])
        second_stage(0, half_m)
        quantize_z(1, half_m, half_m, z_rows1[1])
        second_stage(half_m, half_m)
